import numpy as np
import ml_dtypes


def mxq(x, axis, fmt="e4m3"):
    dtype, down = {"e4m3": (ml_dtypes.float8_e4m3fn, 7), "e5m2": (ml_dtypes.float8_e5m2, 14)}[fmt]
    v = np.moveaxis(np.asarray(x, np.float32).astype(ml_dtypes.bfloat16).astype(np.float64), axis, -1)
    blocks = v.reshape(v.shape[:-1] + (-1, 32))
    amax = np.abs(blocks).max(-1, keepdims=True)
    byte = np.maximum(np.where(amax > 0, np.frexp(amax)[1] - 1 + 127, 0) - down, 1)
    scale = np.exp2(byte - 127.0)
    codes = (blocks / scale).astype(np.float32).astype(dtype).astype(np.float64)
    return np.moveaxis((codes * scale).reshape(v.shape), -1, axis)


WIDE = False


def mx_kscale(k):
    if not WIDE:
        return np.ones(k)
    levels = np.array([10, -10, 5, -5, 0])
    if k % 512:
        return np.exp2(np.random.permutation(np.resize(levels, k // 32))).repeat(32)
    a = np.empty((k // 512, 16))
    for p in range(k // 512):
        a[p, :8] = np.random.permutation(np.resize(levels, 8))
        for g in range(8):
            far = levels[np.abs(levels - a[p, g]) >= 10]
            a[p, g + 8] = far[np.random.randint(len(far))]
    return np.exp2(a.ravel()).repeat(32)


def f64(x):
    return np.asarray(x).astype(np.float64)


def striped(idx):
    return np.tile(idx.reshape(-1, 16).T, (8, 1)).astype(np.uint16)


def unstriped(offs):
    return offs[:16].T.reshape(-1).astype(np.int64)


def pack_weight(w):
    k, n = w.shape
    w = f64(np.asarray(w, np.float32).astype(ml_dtypes.bfloat16)).reshape(k // 32, 32, n)
    amax = np.abs(w).max(1)
    byte = np.clip(np.where(amax > 0, np.frexp(amax)[1] - 1 + 127 - 7, 1), 1, 254)
    scaled = (w * np.exp2(127.0 - byte)[:, None, :]).reshape(k, n).astype(np.float32)
    words = np.ascontiguousarray(scaled.reshape(k // 512, 128, 4, n).transpose(0, 1, 3, 2)).astype(ml_dtypes.float8_e4m3fn).view(np.uint8)
    return words, np.ascontiguousarray(byte.astype(np.uint8).reshape(k // 512, 16, n))


def unpack_weight(words, scales):
    g, p, n, _ = words.shape
    vals = np.ascontiguousarray(words).view(ml_dtypes.float8_e4m3fn).astype(np.float64) * np.repeat(np.exp2(scales.astype(np.float64) - 127.0), 8, axis=1)[..., None]
    return vals.transpose(0, 1, 3, 2).reshape(g * 512, n)


def gelu(v):
    return 0.5 * v * (1.0 + np.tanh(np.sqrt(2.0 / np.pi) * (v + 0.044715 * v**3)))


K, T, S, H, N = 512, 2048, 512, 512, 256


def setup_inputs():
    n = np.random.standard_normal
    s = mx_kscale(K)[:, None]
    u = mx_kscale(H)
    packed_xT = pack_weight(n((K, T)) * s)
    return {
        "x_words": packed_xT[0],
        "x_scales": packed_xT[1],
        "w1": (n((K, H)) / np.sqrt(K) / s * u).astype(np.float32),
        "w2": (n((K, H)) / np.sqrt(K) / s).astype(np.float32),
        "w3": (n((K, H)) / np.sqrt(2 * K) / s * u).astype(np.float32),
        "w4": (n((K, H)) / np.sqrt(2 * K) / s * u).astype(np.float32),
        "w5": (n((H, N)) / np.sqrt(2 * H) / u[:, None]).astype(np.float32),
        "w6": (n((H, N)) / np.sqrt(2 * H) / u[:, None]).astype(np.float32),
        "offs": striped(np.random.permutation(T)[:S]),
        "end": striped(np.random.permutation(T)[:S]),
    }


def reference(x_words, x_scales, w1, w2, w3, w4, w5, w6, offs, end):
    xq = unpack_weight(x_words, x_scales)[:, unstriped(offs)]
    y = mxq(f64(w1), 0, "e4m3").T @ xq
    x_end = unpack_weight(x_words, x_scales)[:, unstriped(end)]
    e = mxq(f64(w2), 0, "e4m3").T @ x_end
    z = y * e
    g = gelu(mxq(f64(w3), 0, "e4m3").T @ xq + mxq(f64(w4), 0, "e4m3").T @ x_end)
    return mxq(f64(w5), 0, "e4m3").T @ mxq(z, 0, "e4m3") + mxq(f64(w6), 0, "e4m3").T @ mxq(g, 0, "e4m3")

@@ -1,0 +1,211 @@
+from contextlib import ExitStack
+
+import concourse.mybir as mybir
+
+K, T, S, H, N = 512, 2048, 512, 512, 256
+FLOPS = 2 * S * (4 * K * H + 2 * H * N)
+
+F32 = mybir.dt.float32
+BF16 = mybir.dt.bfloat16
+I32 = mybir.dt.int32
+U32 = mybir.dt.uint32
+U16 = mybir.dt.uint16
+U8 = mybir.dt.uint8
+FP8X4 = mybir.dt.float8_e4m3fn_x4
+GELU = mybir.ActivationFunctionType.Gelu_apprx_tanh
+MULT = mybir.AluOpType.mult
+
+P = 128
+PACK = 4
+SPANS = 128
+CHUNKS = S // SPANS
+HALF = H // 2
+
+
+def tile_picked_zspan_gelu_p_kernel(tc, x_words, x_scales, w1, w2, w3, w4, w5, w6, offs, end, out):
+    nc = tc.nc
+    with ExitStack() as ctx:
+        keep = ctx.enter_context(tc.tile_pool(name="keep", bufs=1))
+        psum = ctx.enter_context(tc.psum_pool(name="psum", bufs=2))
+
+        def copy_on(engine, out_ap, in_ap):
+            if engine == "vector":
+                nc.vector.tensor_copy(out=out_ap, in_=in_ap)
+            elif engine == "gpsimd":
+                nc.gpsimd.tensor_copy(out=out_ap, in_=in_ap)
+            else:
+                nc.scalar.copy(out=out_ap, in_=in_ap)
+
+        def mx_tiles(name, width):
+            codes = keep.tile([P, width], U32, name=name + "_codes", align_bytes=64)
+            scales = keep.tile([P, width], U8, name=name + "_scales", align_bytes=64)
+            return codes, scales
+
+        def quantise(operand, values):
+            nc.vector.quantize_mx(out=operand[0][:].bitcast(FP8X4), scales=operand[1][:], in_=values)
+
+        def product(acc, pairs):
+            for i, (lhs, lcols, rhs, rcols) in enumerate(pairs):
+                nc.tensor.matmul_mx(
+                    out=acc,
+                    lhsT=lhs[0][:, lcols].bitcast(FP8X4),
+                    lhsT_scale=lhs[1][:, lcols],
+                    rhs=rhs[0][:, rcols].bitcast(FP8X4),
+                    rhs_scale=rhs[1][:, rcols],
+                    start=(i == 0),
+                    stop=(i == len(pairs) - 1),
+                )
+
+        def load_columns(name, w, half):
+            raw = keep.tile([P, PACK, HALF], F32, name="%s_raw%d" % (name, half), tag="%s_raw%d" % (name, half))
+            nc.sync.dma_start(out=raw[:], in_=w[:, half * HALF : (half + 1) * HALF].rearrange("(p j) c -> p j c", j=PACK))
+            return raw
+
+        def round_first(engine, rounded, raw, half):
+            rows = HALF // PACK
+            copy_on(
+                engine,
+                rounded[:, :, half * rows : (half + 1) * rows, :].rearrange("p t m j -> p m j t"),
+                raw[:].rearrange("p j (m t) -> p m j t", t=PACK),
+            )
+
+        def round_second(engine, rounded, raw):
+            copy_on(
+                engine,
+                rounded[:].rearrange("p (c i) j -> p c j i", i=PACK),
+                raw[:].rearrange("p j (c i) -> p c j i", i=PACK),
+            )
+
+        def block(i):
+            return slice(i * P, (i + 1) * P)
+
+        table_words = keep.tile([P, T], I32)
+        table_scales = keep.tile([P, T], U8)
+        start_list = keep.tile([P, S // 16], U16)
+        end_list = keep.tile([P, S // 16], U16)
+        warm_in = keep.tile([P, 8], F32)
+        warm_out = keep.tile([P, 8], F32)
+        rounded = {}
+        mx = {}
+        raws = {}
+        for name in ("w1", "w2", "w3", "w4"):
+            rounded[name] = keep.tile([P, PACK, P, PACK], BF16, name=name + "_rounded", align_bytes=64)
+            mx[name] = mx_tiles(name, H)
+        for name in ("w5", "w6"):
+            rounded[name] = keep.tile([P, N, PACK], BF16, name=name + "_rounded", align_bytes=64)
+            mx[name] = mx_tiles(name, N)
+        mx["xs"] = mx_tiles("xs", S)
+        mx["xe"] = mx_tiles("xe", S)
+        dram = {"w1": w1, "w2": w2, "w3": w3, "w4": w4, "w5": w5, "w6": w6}
+        y_sb = []
+        z_bf = [keep.tile([P, SPANS, PACK], BF16, name="z_bf%d" % c, align_bytes=64) for c in range(CHUNKS)]
+        g_bf = [keep.tile([P, SPANS, PACK], BF16, name="g_bf%d" % c, align_bytes=64) for c in range(CHUNKS)]
+        z_mx = [mx_tiles("z%d" % c, SPANS) for c in range(CHUNKS)]
+        g_mx = [mx_tiles("g%d" % c, SPANS) for c in range(CHUNKS)]
+        out_view = out.rearrange("(h p) s -> p h s", p=P)
+
+        def load_table_words(pieces):
+            words = x_words[0].rearrange("p n r -> p (n r)").bitcast(I32)
+            width = T // pieces
+            for i in range(pieces):
+                nc.sync.dma_start(out=table_words[:, i * width : (i + 1) * width], in_=words[:, i * width : (i + 1) * width])
+
+        def load_table_scales(queue):
+            rows = x_scales[0].rearrange("(q r) n -> r q n", r=PACK)
+            for r in range(PACK):
+                queue.dma_start(out=table_scales[r:P:32, :].bitcast(I32), in_=rows[r].bitcast(I32))
+
+        def load_lists():
+            nc.sync.dma_start(start_list[:], offs)
+            nc.sync.dma_start(end_list[:], end)
+
+        def load(name):
+            for half in range(dram[name].shape[1] // HALF):
+                raws[name, half] = load_columns(name, dram[name], half)
+
+        def gather_scales(name, offsets):
+            nc.vector.tensor_copy(mx[name][1][:], table_scales[:].indirect(offsets[:]))
+
+        def gather_words(name, offsets):
+            nc.vector.tensor_copy(mx[name][0][:], table_words[:].bitcast(U32).indirect(offsets[:]))
+
+        def cast(name, half, engine):
+            if name in ("w5", "w6"):
+                round_second(engine, rounded[name], raws[name, 0])
+            else:
+                round_first(engine, rounded[name], raws[name, half], half)
+
+        def quantise_weight(name):
+            if name in ("w5", "w6"):
+                quantise(mx[name], rounded[name][:].rearrange("p n j -> p (n j)"))
+            else:
+                quantise(mx[name], rounded[name][:].rearrange("p t m j -> p (t m j)"))
+
+        def hidden_bank(tag, terms, c):
+            bank = psum.tile([P, PACK, SPANS], F32, name=tag, bufs=3)
+            for t in range(PACK):
+                product(bank[:, t, :], [(mx[w], block(t), mx[x], block(c)) for w, x in terms])
+            return bank[:].rearrange("p t s -> p s t")
+
+        def do_y(c):
+            nc.scalar.copy(out=y_sb[0][:, block(c), :], in_=hidden_bank("a_bank", [("w1", "xs")], c))
+
+        def do_z(c):
+            nc.vector.tensor_tensor(out=z_bf[c][:], in0=hidden_bank("e_bank", [("w2", "xe")], c), in1=y_sb[0][:, block(c), :], op=MULT)
+
+        def do_g(c):
+            nc.scalar.activation(out=g_bf[c][:], in_=hidden_bank("a_bank", [("w3", "xs"), ("w4", "xe")], c), func=GELU)
+
+        def q_z(c):
+            quantise(z_mx[c], z_bf[c][:].rearrange("p s t -> p (s t)"))
+
+        def q_g(c):
+            quantise(g_mx[c], g_bf[c][:].rearrange("p s t -> p (s t)"))
+
+        def do_out(c, engine):
+            bank = psum.tile([P, N // P, SPANS], F32, name="out_bank")
+            for h in range(N // P):
+                product(bank[:, h, :], [(mx["w6"], block(h), g_mx[c], block(0)), (mx["w5"], block(h), z_mx[c], block(0))])
+            result = keep.tile([P, N // P, SPANS], F32, name="result%d" % c)
+            copy_on(engine, result[:], bank[:])
+            nc.sync.dma_start(out=out_view[:, :, c * SPANS : (c + 1) * SPANS], in_=result[:])
+
+        nc.gpsimd.memset(table_scales[:].bitcast(I32), 0)
+        nc.gpsimd.memset(warm_in[:], 0.0)
+        nc.scalar.activation(out=warm_out[:], in_=warm_in[:], func=GELU)
+        load_lists()
+        load_table_scales(nc.sync)
+        load_table_words(1)
+        for name in ("w1", "w2", "w3", "w4", "w5", "w6"):
+            load(name)
+        gather_scales("xs", start_list)
+        gather_scales("xe", end_list)
+        gather_words("xs", start_list)
+        gather_words("xe", end_list)
+        cast("w1", 0, "scalar")
+        cast("w1", 1, "scalar")
+        quantise_weight("w1")
+        cast("w2", 0, "scalar")
+        cast("w2", 1, "vector")
+        quantise_weight("w2")
+        cast("w3", 0, "vector")
+        cast("w3", 1, "vector")
+        quantise_weight("w3")
+        cast("w4", 0, "scalar")
+        cast("w4", 1, "vector")
+        quantise_weight("w4")
+        y_sb.append(keep.tile([P, S, PACK], F32, name="y_all"))
+        for c in range(CHUNKS):
+            do_y(c)
+            do_z(c)
+        for c in range(CHUNKS):
+            do_g(c)
+        cast("w5", 0, "scalar")
+        cast("w6", 0, "vector")
+        quantise_weight("w5")
+        quantise_weight("w6")
+        for c in range(CHUNKS):
+            q_z(c)
+        for c in range(CHUNKS):
+            q_g(c)
+            do_out(c, "scalar")

@@ -72,7 +72,7 @@ def tile_picked_zspan_gelu_p_kernel(tc, x_words, x_scales, w1, w2, w3, w4, w5, w
         def round_second(engine, rounded, raw):
             copy_on(
                 engine,
-                rounded[:].rearrange("p (c i) j -> p c j i", i=PACK),
+                rounded.rearrange("p (c i) j -> p c j i", i=PACK),
                 raw[:].rearrange("p j (c i) -> p c j i", i=PACK),
             )
 
@@ -89,25 +89,24 @@ def tile_picked_zspan_gelu_p_kernel(tc, x_words, x_scales, w1, w2, w3, w4, w5, w
         mx = {}
         raws = {}
         for name in ("w1", "w2", "w3", "w4"):
-            rounded[name] = keep.tile([P, PACK, P, PACK], BF16, name=name + "_rounded", align_bytes=64)
+            rounded[name] = keep.tile([P, PACK, P, PACK], BF16, name=name + "_rounded", tag=name + "_rounded", align_bytes=64)
             mx[name] = mx_tiles(name, H)
-        for name in ("w5", "w6"):
-            rounded[name] = keep.tile([P, N, PACK], BF16, name=name + "_rounded", align_bytes=64)
-            mx[name] = mx_tiles(name, N)
+        rounded["w56"] = keep.tile([P, 2 * N, PACK], BF16, name="w56_rounded", align_bytes=64)
+        mx["w56"] = mx_tiles("w56", 2 * N)
         mx["xs"] = mx_tiles("xs", S)
         mx["xe"] = mx_tiles("xe", S)
         dram = {"w1": w1, "w2": w2, "w3": w3, "w4": w4, "w5": w5, "w6": w6}
         y_sb = []
-        z_bf = [keep.tile([P, SPANS, PACK], BF16, name="z_bf%d" % c, align_bytes=64) for c in range(CHUNKS)]
+        z_bf = []
         g_bf = [keep.tile([P, SPANS, PACK], BF16, name="g_bf%d" % c, align_bytes=64) for c in range(CHUNKS)]
-        z_mx = [mx_tiles("z%d" % c, SPANS) for c in range(CHUNKS)]
+        z_mx = [mx_tiles("z%d" % c, 2 * SPANS) for c in range(CHUNKS // 2)]
         g_mx = [mx_tiles("g%d" % c, SPANS) for c in range(CHUNKS)]
         out_view = out.rearrange("(h p) s -> p h s", p=P)
 
-        def load_table_words(pieces):
+        def load_table_words(pieces, which):
             words = x_words[0].rearrange("p n r -> p (n r)").bitcast(I32)
             width = T // pieces
-            for i in range(pieces):
+            for i in which:
                 nc.sync.dma_start(out=table_words[:, i * width : (i + 1) * width], in_=words[:, i * width : (i + 1) * width])
 
         def load_table_scales(queue):
@@ -131,18 +130,19 @@ def tile_picked_zspan_gelu_p_kernel(tc, x_words, x_scales, w1, w2, w3, w4, w5, w
 
         def cast(name, half, engine):
             if name in ("w5", "w6"):
-                round_second(engine, rounded[name], raws[name, 0])
+                first = N * ("w5", "w6").index(name)
+                round_second(engine, rounded["w56"][:, first : first + N, :], raws[name, 0])
             else:
                 round_first(engine, rounded[name], raws[name, half], half)
 
         def quantise_weight(name):
-            if name in ("w5", "w6"):
+            if name == "w56":
                 quantise(mx[name], rounded[name][:].rearrange("p n j -> p (n j)"))
             else:
                 quantise(mx[name], rounded[name][:].rearrange("p t m j -> p (t m j)"))
 
         def hidden_bank(tag, terms, c):
-            bank = psum.tile([P, PACK, SPANS], F32, name=tag, bufs=3)
+            bank = psum.tile([P, PACK, SPANS], F32, name=tag, bufs={"a_bank": 4, "e_bank": 2}[tag])
             for t in range(PACK):
                 product(bank[:, t, :], [(mx[w], block(t), mx[x], block(c)) for w, x in terms])
             return bank[:].rearrange("p t s -> p s t")
@@ -151,7 +151,7 @@ def tile_picked_zspan_gelu_p_kernel(tc, x_words, x_scales, w1, w2, w3, w4, w5, w
             nc.scalar.copy(out=y_sb[0][:, block(c), :], in_=hidden_bank("a_bank", [("w1", "xs")], c))
 
         def do_z(c):
-            nc.vector.tensor_tensor(out=z_bf[c][:], in0=hidden_bank("e_bank", [("w2", "xe")], c), in1=y_sb[0][:, block(c), :], op=MULT)
+            nc.vector.tensor_tensor(out=z_bf[c // 2][:, block(c % 2), :], in0=hidden_bank("e_bank", [("w2", "xe")], c), in1=y_sb[0][:, block(c), :], op=MULT)
 
         def do_g(c):
             nc.scalar.activation(out=g_bf[c][:], in_=hidden_bank("a_bank", [("w3", "xs"), ("w4", "xe")], c), func=GELU)
@@ -163,9 +163,9 @@ def tile_picked_zspan_gelu_p_kernel(tc, x_words, x_scales, w1, w2, w3, w4, w5, w
             quantise(g_mx[c], g_bf[c][:].rearrange("p s t -> p (s t)"))
 
         def do_out(c, engine):
-            bank = psum.tile([P, N // P, SPANS], F32, name="out_bank")
+            bank = psum.tile([P, N // P, SPANS], F32, name="out_bank", tag=("out_bank", "e_bank")[c // 2], bufs=2)
             for h in range(N // P):
-                product(bank[:, h, :], [(mx["w6"], block(h), g_mx[c], block(0)), (mx["w5"], block(h), z_mx[c], block(0))])
+                product(bank[:, h, :], [(mx["w56"], block(h), z_mx[c // 2], block(c % 2)), (mx["w56"], block(N // P + h), g_mx[c], block(0))])
             result = keep.tile([P, N // P, SPANS], F32, name="result%d" % c)
             copy_on(engine, result[:], bank[:])
             nc.sync.dma_start(out=out_view[:, :, c * SPANS : (c + 1) * SPANS], in_=result[:])
@@ -173,9 +173,10 @@ def tile_picked_zspan_gelu_p_kernel(tc, x_words, x_scales, w1, w2, w3, w4, w5, w
         nc.gpsimd.memset(table_scales[:].bitcast(I32), 0)
         nc.gpsimd.memset(warm_in[:], 0.0)
         nc.scalar.activation(out=warm_out[:], in_=warm_in[:], func=GELU)
+        load_table_words(2, [0])
         load_lists()
         load_table_scales(nc.sync)
-        load_table_words(1)
+        load_table_words(2, [1])
         for name in ("w1", "w2", "w3", "w4", "w5", "w6"):
             load(name)
         gather_scales("xs", start_list)
@@ -189,23 +190,24 @@ def tile_picked_zspan_gelu_p_kernel(tc, x_words, x_scales, w1, w2, w3, w4, w5, w
         cast("w2", 1, "vector")
         quantise_weight("w2")
         cast("w3", 0, "vector")
-        cast("w3", 1, "vector")
+        cast("w3", 1, "scalar")
         quantise_weight("w3")
-        cast("w4", 0, "scalar")
-        cast("w4", 1, "vector")
+        cast("w4", 0, "vector")
+        cast("w4", 1, "scalar")
         quantise_weight("w4")
+        cast("w5", 0, "scalar")
+        cast("w6", 0, "vector")
+        quantise_weight("w56")
         y_sb.append(keep.tile([P, S, PACK], F32, name="y_all"))
+        z_bf.append(keep.tile([P, 2 * SPANS, PACK], BF16, name="z_first", align_bytes=64))
+        z_bf.append(keep.tile([P, 2 * SPANS, PACK], BF16, name="z_second", tag="w4_rounded", align_bytes=64))
         for c in range(CHUNKS):
             do_y(c)
             do_z(c)
+            if c % 2:
+                q_z(c // 2)
         for c in range(CHUNKS):
             do_g(c)
-        cast("w5", 0, "scalar")
-        cast("w6", 0, "vector")
-        quantise_weight("w5")
-        quantise_weight("w6")
-        for c in range(CHUNKS):
-            q_z(c)
         for c in range(CHUNKS):
             q_g(c)
-            do_out(c, "scalar")
+            do_out(c, ("scalar", "scalar", "vector", "scalar")[c])

@@ -44,29 +44,25 @@ def tile_picked_zspan_gelu_p_kernel(tc, x_words, x_scales, w1, w2, w3, w4, w5, w
         def quantise(operand, values):
             nc.vector.quantize_mx(out=operand[0][:].bitcast(FP8X4), scales=operand[1][:], in_=values)
 
-        def product(acc, pairs):
-            for i, (lhs, lcols, rhs, rcols) in enumerate(pairs):
-                nc.tensor.matmul_mx(
-                    out=acc,
-                    lhsT=lhs[0][:, lcols].bitcast(FP8X4),
-                    lhsT_scale=lhs[1][:, lcols],
-                    rhs=rhs[0][:, rcols].bitcast(FP8X4),
-                    rhs_scale=rhs[1][:, rcols],
-                    start=(i == 0),
-                    stop=(i == len(pairs) - 1),
-                )
+        def load(name, first, last):
+            raw = keep.tile([P, PACK, last - first], F32, name="%s_raw%d" % (name, first), tag="%s_raw%d" % (name, first), align_bytes=64)
+            nc.sync.dma_start(out=raw[:], in_=dram[name][:, first:last].rearrange("(p j) c -> p j c", j=PACK))
+            raws[name, first] = raw
 
-        def load_columns(name, w, half):
-            raw = keep.tile([P, PACK, HALF], F32, name="%s_raw%d" % (name, half), tag="%s_raw%d" % (name, half))
-            nc.sync.dma_start(out=raw[:], in_=w[:, half * HALF : (half + 1) * HALF].rearrange("(p j) c -> p j c", j=PACK))
-            return raw
-
-        def round_first(engine, rounded, raw, half):
-            rows = HALF // PACK
+        def cast(name, first, slots, engine):
+            raw = raws[name, first]
             copy_on(
                 engine,
-                rounded[:, :, half * rows : (half + 1) * rows, :].rearrange("p t m j -> p m j t"),
-                raw[:].rearrange("p j (m t) -> p m j t", t=PACK),
+                rounded[name][:, slots, first // PACK : (first + raw.shape[2]) // PACK, :].rearrange("p t m j -> p m j t"),
+                raw[:].rearrange("p j (m t) -> p m j t", t=PACK)[:, :, :, slots],
+            )
+
+        def quantise_pair(name, pair):
+            cols = slice(pair * HALF, (pair + 1) * HALF)
+            nc.vector.quantize_mx(
+                out=mx[name][0][:, cols].bitcast(FP8X4),
+                scales=mx[name][1][:, cols],
+                in_=rounded[name][:, 2 * pair : 2 * pair + 2, :, :].rearrange("p t m j -> p (t m j)"),
             )
 
         def round_second(engine, rounded, raw):
@@ -91,16 +87,15 @@ def tile_picked_zspan_gelu_p_kernel(tc, x_words, x_scales, w1, w2, w3, w4, w5, w
         for name in ("w1", "w2", "w3", "w4"):
             rounded[name] = keep.tile([P, PACK, P, PACK], BF16, name=name + "_rounded", tag=name + "_rounded", align_bytes=64)
             mx[name] = mx_tiles(name, H)
-        rounded["w56"] = keep.tile([P, 2 * N, PACK], BF16, name="w56_rounded", align_bytes=64)
-        mx["w56"] = mx_tiles("w56", 2 * N)
+        for name in ("w5", "w6"):
+            rounded[name] = keep.tile([P, N, PACK], BF16, name=name + "_rounded", tag=name + "_rounded", align_bytes=64)
+            mx[name] = mx_tiles(name, N)
         mx["xs"] = mx_tiles("xs", S)
         mx["xe"] = mx_tiles("xe", S)
         dram = {"w1": w1, "w2": w2, "w3": w3, "w4": w4, "w5": w5, "w6": w6}
-        y_sb = []
-        z_bf = []
-        g_bf = [keep.tile([P, SPANS, PACK], BF16, name="g_bf%d" % c, align_bytes=64) for c in range(CHUNKS)]
-        z_mx = [mx_tiles("z%d" % c, 2 * SPANS) for c in range(CHUNKS // 2)]
-        g_mx = [mx_tiles("g%d" % c, SPANS) for c in range(CHUNKS)]
+        y_sb = {}
+        z_bf = {}
+        g_bf = {}
         out_view = out.rearrange("(h p) s -> p h s", p=P)
 
         def load_table_words(pieces, which):
@@ -118,54 +113,70 @@ def tile_picked_zspan_gelu_p_kernel(tc, x_words, x_scales, w1, w2, w3, w4, w5, w
             nc.sync.dma_start(start_list[:], offs)
             nc.sync.dma_start(end_list[:], end)
 
-        def load(name):
-            for half in range(dram[name].shape[1] // HALF):
-                raws[name, half] = load_columns(name, dram[name], half)
-
         def gather_scales(name, offsets):
             nc.vector.tensor_copy(mx[name][1][:], table_scales[:].indirect(offsets[:]))
 
         def gather_words(name, offsets):
             nc.vector.tensor_copy(mx[name][0][:], table_words[:].bitcast(U32).indirect(offsets[:]))
 
-        def cast(name, half, engine):
-            if name in ("w5", "w6"):
-                first = N * ("w5", "w6").index(name)
-                round_second(engine, rounded["w56"][:, first : first + N, :], raws[name, 0])
-            else:
-                round_first(engine, rounded[name], raws[name, half], half)
+        def cast_second(name, engine):
+            round_second(engine, rounded[name][:], raws[name, 0])
 
         def quantise_weight(name):
-            if name == "w56":
+            if name in ("w5", "w6"):
                 quantise(mx[name], rounded[name][:].rearrange("p n j -> p (n j)"))
             else:
                 quantise(mx[name], rounded[name][:].rearrange("p t m j -> p (t m j)"))
 
-        def hidden_bank(tag, terms, c):
-            bank = psum.tile([P, PACK, SPANS], F32, name=tag, bufs={"a_bank": 4, "e_bank": 2}[tag])
+        def new_bank(number, shape):
+            return psum.tile(shape, F32, name="bank%d" % number, tag="bank%d" % number, bufs=1)
+
+        def one_pass(acc, lhs, lcols, rhs, rcols, start, stop):
+            nc.tensor.matmul_mx(
+                out=acc,
+                lhsT=lhs[0][:, lcols].bitcast(FP8X4),
+                lhsT_scale=lhs[1][:, lcols],
+                rhs=rhs[0][:, rcols].bitcast(FP8X4),
+                rhs_scale=rhs[1][:, rcols],
+                start=start,
+                stop=stop,
+            )
+
+        def hidden_bank(number, w, x, c):
+            bank = new_bank(number, [P, PACK, SPANS])
             for t in range(PACK):
-                product(bank[:, t, :], [(mx[w], block(t), mx[x], block(c)) for w, x in terms])
+                one_pass(bank[:, t, :], mx[w], block(t), mx[x], block(c), True, True)
             return bank[:].rearrange("p t s -> p s t")
 
         def do_y(c):
-            nc.scalar.copy(out=y_sb[0][:, block(c), :], in_=hidden_bank("a_bank", [("w1", "xs")], c))
+            nc.scalar.copy(out=y_sb[c], in_=hidden_bank((0, 1, 2, 3)[c], "w1", "xs", c))
 
         def do_z(c):
-            nc.vector.tensor_tensor(out=z_bf[c // 2][:, block(c % 2), :], in0=hidden_bank("e_bank", [("w2", "xe")], c), in1=y_sb[0][:, block(c), :], op=MULT)
+            nc.vector.tensor_tensor(out=z_bf[c], in0=hidden_bank((2, 3, 0, 1)[c], "w2", "xe", c), in1=y_sb[c], op=MULT)
 
-        def do_g(c):
-            nc.scalar.activation(out=g_bf[c][:], in_=hidden_bank("a_bank", [("w3", "xs"), ("w4", "xe")], c), func=GELU)
+        def open_g(c):
+            bank = new_bank(4 + c, [P, PACK, SPANS])
+            one_pass(bank[:, 0, :], mx["w3"], block(0), mx["xs"], block(c), True, False)
+            return bank
 
-        def q_z(c):
-            quantise(z_mx[c], z_bf[c][:].rearrange("p s t -> p (s t)"))
+        def do_g(c, bank):
+            for t in range(PACK):
+                if t:
+                    one_pass(bank[:, t, :], mx["w3"], block(t), mx["xs"], block(c), True, False)
+                one_pass(bank[:, t, :], mx["w4"], block(t), mx["xe"], block(c), False, True)
+            nc.scalar.activation(out=g_bf[c], in_=bank[:].rearrange("p t s -> p s t"), func=GELU)
 
-        def q_g(c):
-            quantise(g_mx[c], g_bf[c][:].rearrange("p s t -> p (s t)"))
+        def q_cols(name, first, values):
+            cols = slice(first * SPANS, first * SPANS + values.shape[1])
+            nc.vector.quantize_mx(
+                out=mx[name][0][:, cols].bitcast(FP8X4), scales=mx[name][1][:, cols], in_=values.rearrange("p s t -> p (s t)")
+            )
 
         def do_out(c, engine):
-            bank = psum.tile([P, N // P, SPANS], F32, name="out_bank", tag=("out_bank", "e_bank")[c // 2], bufs=2)
+            bank = new_bank((2, 3, 0, 1)[c], [P, N // P, SPANS])
             for h in range(N // P):
-                product(bank[:, h, :], [(mx["w56"], block(h), z_mx[c // 2], block(c % 2)), (mx["w56"], block(N // P + h), g_mx[c], block(0))])
+                one_pass(bank[:, h, :], mx["w5"], block(h), mx["z"], block(c), True, False)
+                one_pass(bank[:, h, :], mx["w6"], block(h), mx["g"], block(c), False, True)
             result = keep.tile([P, N // P, SPANS], F32, name="result%d" % c)
             copy_on(engine, result[:], bank[:])
             nc.sync.dma_start(out=out_view[:, :, c * SPANS : (c + 1) * SPANS], in_=result[:])
@@ -177,37 +188,61 @@ def tile_picked_zspan_gelu_p_kernel(tc, x_words, x_scales, w1, w2, w3, w4, w5, w
         load_lists()
         load_table_scales(nc.sync)
         load_table_words(2, [1])
-        for name in ("w1", "w2", "w3", "w4", "w5", "w6"):
-            load(name)
+        load("w1", 0, HALF)
+        load("w1", HALF, H)
+        for name in ("w2", "w3", "w4"):
+            load(name, 0, H)
+        for name in ("w5", "w6"):
+            load(name, 0, N)
         gather_scales("xs", start_list)
         gather_scales("xe", end_list)
         gather_words("xs", start_list)
         gather_words("xe", end_list)
-        cast("w1", 0, "scalar")
-        cast("w1", 1, "scalar")
+        cast("w1", 0, slice(0, 4), "scalar")
+        cast("w1", HALF, slice(0, 4), "scalar")
         quantise_weight("w1")
-        cast("w2", 0, "scalar")
-        cast("w2", 1, "vector")
-        quantise_weight("w2")
-        cast("w3", 0, "vector")
-        cast("w3", 1, "scalar")
-        quantise_weight("w3")
-        cast("w4", 0, "vector")
-        cast("w4", 1, "scalar")
-        quantise_weight("w4")
-        cast("w5", 0, "scalar")
-        cast("w6", 0, "vector")
-        quantise_weight("w56")
-        y_sb.append(keep.tile([P, S, PACK], F32, name="y_all"))
-        z_bf.append(keep.tile([P, 2 * SPANS, PACK], BF16, name="z_first", align_bytes=64))
-        z_bf.append(keep.tile([P, 2 * SPANS, PACK], BF16, name="z_second", tag="w4_rounded", align_bytes=64))
+        for name in ("w2", "w3", "w4"):
+            cast(name, 0, slice(0, 2), "vector")
+            cast(name, 0, slice(2, 4), "scalar")
+            quantise_pair(name, 0)
+            quantise_pair(name, 1)
+        cast_second("w5", "scalar")
+        cast_second("w6", "vector")
+        quantise_weight("w5")
+        quantise_weight("w6")
+        y_first = keep.tile([P, 2 * SPANS, PACK], F32, tag="w2_raw0", align_bytes=64)
+        y_middle = keep.tile([P, SPANS, PACK], F32, tag="w3_raw0", align_bytes=64)
+        y_last = keep.tile([P, SPANS, PACK], F32, tag="w4_raw0", align_bytes=64)
+        for c, ap in {0: y_first[:, block(0), :], 1: y_first[:, block(1), :], 2: y_middle[:], 3: y_last[:]}.items():
+            y_sb[c] = ap
+        z_first = keep.tile([P, 2 * SPANS, PACK], BF16, align_bytes=64)
+        z_third = keep.tile([P, SPANS, PACK], BF16, tag="w4_rounded", align_bytes=64)
+        z_last = keep.tile([P, SPANS, PACK], BF16, tag="w5_rounded", align_bytes=64)
+        for c, ap in {0: z_first[:, block(0), :], 1: z_first[:, block(1), :], 2: z_third[:], 3: z_last[:]}.items():
+            z_bf[c] = ap
+        g_all = keep.tile([P, S, PACK], BF16, tag="w5_raw0", align_bytes=64)
+        g_codes = keep.tile([P, S], U32, tag="w6_rounded", align_bytes=64)
+        g_scales = keep.tile([P, S], U8, align_bytes=64)
+        mx["g"] = (g_codes, g_scales)
+        z_codes = keep.tile([P, S], U32, tag="w3_rounded", align_bytes=64)
+        z_scales = keep.tile([P, S], U8, align_bytes=64)
+        mx["z"] = (z_codes, z_scales)
         for c in range(CHUNKS):
-            do_y(c)
-            do_z(c)
-            if c % 2:
-                q_z(c // 2)
+            g_bf[c] = g_all[:, block(c), :]
+        do_y(0)
+        do_y(1)
+        do_z(0)
+        do_z(1)
+        g_banks = [open_g(c) for c in range(CHUNKS)]
+        do_y(2)
+        do_y(3)
+        q_cols("z", 0, z_first[:])
+        do_z(2)
+        do_z(3)
+        q_cols("z", 2, z_third[:])
+        q_cols("z", 3, z_last[:])
         for c in range(CHUNKS):
-            do_g(c)
+            do_g(c, g_banks[c])
         for c in range(CHUNKS):
-            q_g(c)
+            q_cols("g", c, g_bf[c])
             do_out(c, ("scalar", "scalar", "vector", "scalar")[c])

from contextlib import ExitStack

import concourse.mybir as mybir

K, T, S, H, N = 512, 2048, 512, 512, 256
FLOPS = 2 * S * (4 * K * H + 2 * H * N)

F32 = mybir.dt.float32
BF16 = mybir.dt.bfloat16
I32 = mybir.dt.int32
U32 = mybir.dt.uint32
U16 = mybir.dt.uint16
U8 = mybir.dt.uint8
FP8X4 = mybir.dt.float8_e4m3fn_x4
GELU = mybir.ActivationFunctionType.Gelu_apprx_tanh
MULT = mybir.AluOpType.mult

P = 128
PACK = 4
SPANS = 128
CHUNKS = S // SPANS
HALF = H // 2


def tile_picked_zspan_gelu_p_kernel(tc, x_words, x_scales, w1, w2, w3, w4, w5, w6, offs, end, out):
    nc = tc.nc
    with ExitStack() as ctx:
        keep = ctx.enter_context(tc.tile_pool(name="keep", bufs=1))
        psum = ctx.enter_context(tc.psum_pool(name="psum", bufs=2))

        def copy_on(engine, out_ap, in_ap):
            if engine == "vector":
                nc.vector.tensor_copy(out=out_ap, in_=in_ap)
            elif engine == "gpsimd":
                nc.gpsimd.tensor_copy(out=out_ap, in_=in_ap)
            else:
                nc.scalar.copy(out=out_ap, in_=in_ap)

        def mx_tiles(name, width):
            codes = keep.tile([P, width], U32, name=name + "_codes", align_bytes=64)
            scales = keep.tile([P, width], U8, name=name + "_scales", align_bytes=64)
            return codes, scales

        def quantise(operand, values):
            nc.vector.quantize_mx(out=operand[0][:].bitcast(FP8X4), scales=operand[1][:], in_=values)

        def load(name, first, last):
            raw = keep.tile([P, PACK, last - first], F32, name="%s_raw%d" % (name, first), tag="%s_raw%d" % (name, first), align_bytes=64)
            nc.sync.dma_start(out=raw[:], in_=dram[name][:, first:last].rearrange("(p j) c -> p j c", j=PACK))
            raws[name, first] = raw

        def cast(name, first, slots, engine):
            raw = raws[name, first]
            copy_on(
                engine,
                rounded[name][:, slots, first // PACK : (first + raw.shape[2]) // PACK, :].rearrange("p t m j -> p m j t"),
                raw[:].rearrange("p j (m t) -> p m j t", t=PACK)[:, :, :, slots],
            )

        def quantise_pair(name, pair):
            cols = slice(pair * HALF, (pair + 1) * HALF)
            nc.vector.quantize_mx(
                out=mx[name][0][:, cols].bitcast(FP8X4),
                scales=mx[name][1][:, cols],
                in_=rounded[name][:, 2 * pair : 2 * pair + 2, :, :].rearrange("p t m j -> p (t m j)"),
            )

        def round_second(engine, rounded, raw):
            copy_on(
                engine,
                rounded.rearrange("p (c i) j -> p c j i", i=PACK),
                raw[:].rearrange("p j (c i) -> p c j i", i=PACK),
            )

        def block(i):
            return slice(i * P, (i + 1) * P)

        table_words = keep.tile([P, T], I32)
        table_scales = keep.tile([P, T], U8)
        start_list = keep.tile([P, S // 16], U16)
        end_list = keep.tile([P, S // 16], U16)
        warm_in = keep.tile([P, 8], F32)
        warm_out = keep.tile([P, 8], F32)
        rounded = {}
        mx = {}
        raws = {}
        for name in ("w1", "w2", "w3", "w4"):
            rounded[name] = keep.tile([P, PACK, P, PACK], BF16, name=name + "_rounded", tag=name + "_rounded", align_bytes=64)
            mx[name] = mx_tiles(name, H)
        for name in ("w5", "w6"):
            rounded[name] = keep.tile([P, N, PACK], BF16, name=name + "_rounded", tag=name + "_rounded", align_bytes=64)
            mx[name] = mx_tiles(name, N)
        mx["xs"] = mx_tiles("xs", S)
        mx["xe"] = mx_tiles("xe", S)
        dram = {"w1": w1, "w2": w2, "w3": w3, "w4": w4, "w5": w5, "w6": w6}
        y_sb = {}
        z_bf = {}
        g_bf = {}
        out_view = out.rearrange("(h p) s -> p h s", p=P)

        def load_table_words(pieces, which):
            words = x_words[0].rearrange("p n r -> p (n r)").bitcast(I32)
            width = T // pieces
            for i in which:
                nc.sync.dma_start(out=table_words[:, i * width : (i + 1) * width], in_=words[:, i * width : (i + 1) * width])

        def load_table_scales(queue):
            rows = x_scales[0].rearrange("(q r) n -> r q n", r=PACK)
            for r in range(PACK):
                queue.dma_start(out=table_scales[r:P:32, :].bitcast(I32), in_=rows[r].bitcast(I32))

        def load_lists():
            nc.sync.dma_start(start_list[:], offs)
            nc.sync.dma_start(end_list[:], end)

        def gather_scales(name, offsets):
            nc.vector.tensor_copy(mx[name][1][:], table_scales[:].indirect(offsets[:]))

        def gather_words(name, offsets):
            nc.vector.tensor_copy(mx[name][0][:], table_words[:].bitcast(U32).indirect(offsets[:]))

        def cast_second(name, engine):
            round_second(engine, rounded[name][:], raws[name, 0])

        def quantise_weight(name):
            if name in ("w5", "w6"):
                quantise(mx[name], rounded[name][:].rearrange("p n j -> p (n j)"))
            else:
                quantise(mx[name], rounded[name][:].rearrange("p t m j -> p (t m j)"))

        def new_bank(number, shape):
            return psum.tile(shape, F32, name="bank%d" % number, tag="bank%d" % number, bufs=1)

        def one_pass(acc, lhs, lcols, rhs, rcols, start, stop):
            nc.tensor.matmul_mx(
                out=acc,
                lhsT=lhs[0][:, lcols].bitcast(FP8X4),
                lhsT_scale=lhs[1][:, lcols],
                rhs=rhs[0][:, rcols].bitcast(FP8X4),
                rhs_scale=rhs[1][:, rcols],
                start=start,
                stop=stop,
            )

        def hidden_bank(number, w, x, c):
            bank = new_bank(number, [P, PACK, SPANS])
            for t in range(PACK):
                one_pass(bank[:, t, :], mx[w], block(t), mx[x], block(c), True, True)
            return bank[:].rearrange("p t s -> p s t")

        def do_y(c):
            nc.scalar.copy(out=y_sb[c], in_=hidden_bank((0, 1, 2, 3)[c], "w1", "xs", c))

        def do_z(c):
            nc.vector.tensor_tensor(out=z_bf[c], in0=hidden_bank((2, 3, 0, 1)[c], "w2", "xe", c), in1=y_sb[c], op=MULT)

        def open_g(c):
            bank = new_bank(4 + c, [P, PACK, SPANS])
            one_pass(bank[:, 0, :], mx["w3"], block(0), mx["xs"], block(c), True, False)
            return bank

        def do_g(c, bank):
            for t in range(PACK):
                if t:
                    one_pass(bank[:, t, :], mx["w3"], block(t), mx["xs"], block(c), True, False)
                one_pass(bank[:, t, :], mx["w4"], block(t), mx["xe"], block(c), False, True)
            nc.scalar.activation(out=g_bf[c], in_=bank[:].rearrange("p t s -> p s t"), func=GELU)

        def q_cols(name, first, values):
            cols = slice(first * SPANS, first * SPANS + values.shape[1])
            nc.vector.quantize_mx(
                out=mx[name][0][:, cols].bitcast(FP8X4), scales=mx[name][1][:, cols], in_=values.rearrange("p s t -> p (s t)")
            )

        def do_out(c, engine):
            bank = new_bank((2, 3, 0, 1)[c], [P, N // P, SPANS])
            for h in range(N // P):
                one_pass(bank[:, h, :], mx["w5"], block(h), mx["z"], block(c), True, False)
                one_pass(bank[:, h, :], mx["w6"], block(h), mx["g"], block(c), False, True)
            result = keep.tile([P, N // P, SPANS], F32, name="result%d" % c)
            copy_on(engine, result[:], bank[:])
            nc.sync.dma_start(out=out_view[:, :, c * SPANS : (c + 1) * SPANS], in_=result[:])

        nc.gpsimd.memset(table_scales[:].bitcast(I32), 0)
        nc.gpsimd.memset(warm_in[:], 0.0)
        nc.scalar.activation(out=warm_out[:], in_=warm_in[:], func=GELU)
        load_table_words(2, [0])
        load_lists()
        load_table_scales(nc.sync)
        load_table_words(2, [1])
        load("w1", 0, HALF)
        load("w1", HALF, H)
        for name in ("w2", "w3", "w4"):
            load(name, 0, H)
        for name in ("w5", "w6"):
            load(name, 0, N)
        gather_scales("xs", start_list)
        gather_scales("xe", end_list)
        gather_words("xs", start_list)
        gather_words("xe", end_list)
        cast("w1", 0, slice(0, 4), "scalar")
        cast("w1", HALF, slice(0, 4), "scalar")
        quantise_weight("w1")
        for name in ("w2", "w3", "w4"):
            cast(name, 0, slice(0, 2), "vector")
            cast(name, 0, slice(2, 4), "scalar")
            quantise_pair(name, 0)
            quantise_pair(name, 1)
        cast_second("w5", "scalar")
        cast_second("w6", "vector")
        quantise_weight("w5")
        quantise_weight("w6")
        y_first = keep.tile([P, 2 * SPANS, PACK], F32, tag="w2_raw0", align_bytes=64)
        y_middle = keep.tile([P, SPANS, PACK], F32, tag="w3_raw0", align_bytes=64)
        y_last = keep.tile([P, SPANS, PACK], F32, tag="w4_raw0", align_bytes=64)
        for c, ap in {0: y_first[:, block(0), :], 1: y_first[:, block(1), :], 2: y_middle[:], 3: y_last[:]}.items():
            y_sb[c] = ap
        z_first = keep.tile([P, 2 * SPANS, PACK], BF16, align_bytes=64)
        z_third = keep.tile([P, SPANS, PACK], BF16, tag="w4_rounded", align_bytes=64)
        z_last = keep.tile([P, SPANS, PACK], BF16, tag="w5_rounded", align_bytes=64)
        for c, ap in {0: z_first[:, block(0), :], 1: z_first[:, block(1), :], 2: z_third[:], 3: z_last[:]}.items():
            z_bf[c] = ap
        g_all = keep.tile([P, S, PACK], BF16, tag="w5_raw0", align_bytes=64)
        g_codes = keep.tile([P, S], U32, tag="w6_rounded", align_bytes=64)
        g_scales = keep.tile([P, S], U8, align_bytes=64)
        mx["g"] = (g_codes, g_scales)
        z_codes = keep.tile([P, S], U32, tag="w3_rounded", align_bytes=64)
        z_scales = keep.tile([P, S], U8, align_bytes=64)
        mx["z"] = (z_codes, z_scales)
        for c in range(CHUNKS):
            g_bf[c] = g_all[:, block(c), :]
        do_y(0)
        do_y(1)
        do_z(0)
        do_z(1)
        g_banks = [open_g(c) for c in range(CHUNKS)]
        do_y(2)
        do_y(3)
        q_cols("z", 0, z_first[:])
        do_z(2)
        do_z(3)
        q_cols("z", 2, z_third[:])
        q_cols("z", 3, z_last[:])
        for c in range(CHUNKS):
            do_g(c, g_banks[c])
        for c in range(CHUNKS):
            q_cols("g", c, g_bf[c])
            do_out(c, ("scalar", "scalar", "vector", "scalar")[c])
